import numpy as np
import ml_dtypes


def mxq(x, axis, fmt="e4m3"):
    dtype, down = {"e4m3": (ml_dtypes.float8_e4m3fn, 7), "e5m2": (ml_dtypes.float8_e5m2, 14)}[fmt]
    v = np.moveaxis(np.asarray(x, np.float32).astype(ml_dtypes.bfloat16).astype(np.float64), axis, -1)
    blocks = v.reshape(v.shape[:-1] + (-1, 32))
    amax = np.abs(blocks).max(-1, keepdims=True)
    byte = np.maximum(np.where(amax > 0, np.frexp(amax)[1] - 1 + 127, 0) - down, 1)
    scale = np.exp2(byte - 127.0)
    codes = (blocks / scale).astype(np.float32).astype(dtype).astype(np.float64)
    return np.moveaxis((codes * scale).reshape(v.shape), -1, axis)


WIDE = False


def mx_kscale(k):
    if not WIDE:
        return np.ones(k)
    levels = np.array([10, -10, 5, -5, 0])
    if k % 512:
        return np.exp2(np.random.permutation(np.resize(levels, k // 32))).repeat(32)
    a = np.empty((k // 512, 16))
    for p in range(k // 512):
        a[p, :8] = np.random.permutation(np.resize(levels, 8))
        for g in range(8):
            far = levels[np.abs(levels - a[p, g]) >= 10]
            a[p, g + 8] = far[np.random.randint(len(far))]
    return np.exp2(a.ravel()).repeat(32)


def f64(x):
    return np.asarray(x).astype(np.float64)


def striped(idx):
    return np.tile(idx.reshape(-1, 16).T, (8, 1)).astype(np.uint16)


def unstriped(offs):
    return offs[:16].T.reshape(-1).astype(np.int64)


def striped8(idx):
    return np.concatenate([x.reshape(-1, 16).T for x in idx]).astype(np.uint16)


def runs(offs, k):
    lists = np.stack([offs[16 * r : 16 * r + 16].T.reshape(-1) for r in range(8)]).astype(np.int64)
    return lists[np.arange(k) % 512 // 64]


def pack_weight(w):
    k, n = w.shape
    w = f64(np.asarray(w, np.float32).astype(ml_dtypes.bfloat16)).reshape(k // 32, 32, n)
    amax = np.abs(w).max(1)
    byte = np.clip(np.where(amax > 0, np.frexp(amax)[1] - 1 + 127 - 7, 1), 1, 254)
    scaled = (w * np.exp2(127.0 - byte)[:, None, :]).reshape(k, n).astype(np.float32)
    words = np.ascontiguousarray(scaled.reshape(k // 512, 128, 4, n).transpose(0, 1, 3, 2)).astype(ml_dtypes.float8_e4m3fn).view(np.uint8)
    return words, np.ascontiguousarray(byte.astype(np.uint8).reshape(k // 512, 16, n))


def unpack_weight(words, scales):
    g, p, n, _ = words.shape
    vals = np.ascontiguousarray(words).view(ml_dtypes.float8_e4m3fn).astype(np.float64) * np.repeat(np.exp2(scales.astype(np.float64) - 127.0), 8, axis=1)[..., None]
    return vals.transpose(0, 1, 3, 2).reshape(g * 512, n)

def planes(y):
    n, m = y.shape
    v = y.astype(np.float32).astype(ml_dtypes.bfloat16).astype(np.float64).reshape(n // 32, 32, m)
    top = np.abs(v).max(1)
    byte = np.clip(np.where(top > 0, np.frexp(top)[1] - 1 + 127 - 7, 1), 1, 254)
    codes = (v * np.exp2(127.0 - byte)[:, None, :]).reshape(n, m).astype(np.float32).astype(ml_dtypes.float8_e4m3fn).view(np.uint8)
    words = codes.reshape(n // 512, 128, 4, m).transpose(0, 1, 3, 2)
    return np.ascontiguousarray(words), np.ascontiguousarray(byte.astype(np.uint8).reshape(n // 512, 16, m))


K, T, S, V, N, H = 512, 2048, 512, 256, 512, 512


def setup_inputs():
    n = np.random.standard_normal
    s = mx_kscale(K)[:, None]
    u = mx_kscale(H)
    packed_xT = pack_weight(n((K, T)) * s)
    packed_w1 = pack_weight(n((K, H)) / np.sqrt(K) / s)
    packed_w2 = pack_weight(n((H, N)) / np.sqrt(H) / u[:, None])
    perm = np.stack([np.random.permutation(S) for _ in range(8)])
    perm2 = np.stack([np.random.permutation(S) for _ in range(8)])
    return {
        "x_words": packed_xT[0],
        "x_scales": packed_xT[1],
        "w1_words": packed_w1[0],
        "w1_scales": packed_w1[1],
        "gn": (np.random.uniform(0.5, 1.5, (H, 1)) * u[:, None]).astype(np.float32),
        "w2_words": packed_w2[0],
        "w2_scales": packed_w2[1],
        "offs": striped(np.random.permutation(T)[:S]),
        "la": striped8(perm[:, :V]),
        "lb": striped8(perm[:, V:]),
        "ma": striped8(perm2[:, :V]),
        "mb": striped8(perm2[:, V:]),
    }


def reference(x_words, x_scales, w1_words, w1_scales, gn, w2_words, w2_scales, offs, la, lb, ma, mb):
    xq = unpack_weight(x_words, x_scales)[:, unstriped(offs)]
    y = unpack_weight(w1_words, w1_scales).T @ xq
    a = y[np.arange(H)[:, None], runs(la, H)]
    b = y[np.arange(H)[:, None], runs(lb, H)]
    pb = a * b
    pa = a + b
    d1 = np.zeros((H, S))
    d1[np.arange(H)[:, None], runs(la, H)] = pa
    d2 = d1.copy()
    d2[np.arange(H)[:, None], runs(lb, H)] = pb
    z = f64(gn) * d2
    h = unpack_weight(w2_words, w2_scales).T @ mxq(z, 0, "e4m3")
    c = h[np.arange(N)[:, None], runs(ma, N)]
    d = h[np.arange(N)[:, None], runs(mb, N)]
    ob = c - d
    oa = np.abs(c + d)
    d3 = np.zeros((N, S))
    d3[np.arange(N)[:, None], runs(ma, N)] = oa
    out = d3.copy()
    out[np.arange(N)[:, None], runs(mb, N)] = ob
    return (out,) + planes(out)

@@ -1,0 +1,200 @@
+from contextlib import ExitStack
+
+import concourse.mybir as mybir
+
+F32 = mybir.dt.float32
+BF16 = mybir.dt.bfloat16
+I32 = mybir.dt.int32
+U32 = mybir.dt.uint32
+U16 = mybir.dt.uint16
+U8 = mybir.dt.uint8
+FP8X4 = mybir.dt.float8_e4m3fn_x4
+ADD = mybir.AluOpType.add
+MULT = mybir.AluOpType.mult
+COPY = mybir.ActivationFunctionType.Copy
+ABS = mybir.ActivationFunctionType.Abs
+
+P = 128
+PACK = 4
+T = 2048
+S = 512
+V = 256
+HALF = S // 2
+FLOPS = 2 * 512 * 512 * 512 * 2
+
+
+def tile_picked_pairpoly_none_po_kernel(
+    tc, x_words, x_scales, w1_words, w1_scales, gn, w2_words, w2_scales, offs, la, lb, ma, mb, out_0, out_1, out_2
+):
+    nc = tc.nc
+    halves = [slice(0, HALF), slice(HALF, S)]
+
+    def as_words(packed):
+        return packed[0].rearrange("p n t -> p (n t)").bitcast(I32)
+
+    def load_scale_rows(queues, plane, rows):
+        for q, queue in enumerate(queues):
+            queue.dma_start(out=plane[32 * q : 32 * q + 4, :].bitcast(I32), in_=rows[0, 4 * q : 4 * q + 4, :].bitcast(I32))
+
+    with ExitStack() as ctx:
+        held = ctx.enter_context(tc.tile_pool(name="held", bufs=1))
+        psum = ctx.enter_context(tc.psum_pool(name="psum", bufs=1))
+
+        def new(name, shape, dtype):
+            return held.tile(shape, dtype, name=name, align_bytes=64)
+
+        offs_sb = new("offs_sb", [P, S // 16], U16)
+        la_sb = new("la_sb", [P, V // 16], U16)
+        lb_sb = new("lb_sb", [P, V // 16], U16)
+        ma_sb = new("ma_sb", [P, V // 16], U16)
+        mb_sb = new("mb_sb", [P, V // 16], U16)
+        x_table = new("x_table", [P, T], U32)
+        x_table_scales = new("x_table_scales", [P, T], U8)
+        w_raw = new("w_raw", [P, S], I32)
+        w_raw_scales = new("w_raw_scales", [P, S], U8)
+        gain = new("gain", [P, PACK], F32)
+
+        nc.vector.memset(x_table_scales[:].bitcast(I32), 0)
+        nc.gpsimd.memset(w_raw_scales[:].bitcast(I32), 0)
+
+        nc.sync.dma_start(offs_sb[:], offs)
+        nc.sync.dma_start(la_sb[:], la)
+        nc.sync.dma_start(lb_sb[:], lb)
+        nc.sync.dma_start(ma_sb[:], ma)
+        nc.sync.dma_start(mb_sb[:], mb)
+        nc.sync.dma_start(out=x_table[:].bitcast(I32), in_=as_words(x_words))
+        nc.sync.dma_start(out=w_raw[:], in_=as_words(w1_words))
+        load_scale_rows([nc.scalar] * 4, x_table_scales, x_scales)
+        load_scale_rows([nc.scalar, nc.scalar, nc.gpsimd, nc.gpsimd], w_raw_scales, w1_scales)
+        nc.gpsimd.dma_start(out=gain[:], in_=gn.rearrange("(p t) o -> p (t o)", t=PACK))
+
+        def deal(name, raw, dtype):
+            dealt = new(name, [P, PACK, P], dtype)
+            nc.vector.tensor_copy(out=dealt[:].rearrange("p t m -> p m t"), in_=raw[:].rearrange("p (m t) -> p m t", t=PACK))
+            return dealt
+
+        x_codes = new("x_codes", [P, S], U32)
+        x_plane = new("x_plane", [P, S], U8)
+        w1_plane = deal("w1_plane", w_raw_scales, U8)
+        nc.vector.tensor_copy(x_plane[:], x_table_scales[:].indirect(offs_sb[:]))
+        nc.vector.tensor_copy(x_codes[:, halves[0]], x_table[:].indirect(offs_sb[:, 0 : HALF // 16]))
+        w1_codes = deal("w1_codes", w_raw, I32)
+        nc.vector.tensor_copy(x_codes[:, halves[1]], x_table[:].indirect(offs_sb[:, HALF // 16 : S // 16]))
+
+        def product(name, w_codes, w_plane, codes, plane, scale):
+            rows = []
+            for t in range(PACK):
+                row = new("%s%d" % (name, t), [P, S], F32)
+                for n, cols in enumerate(halves if t == 0 else [slice(0, S)]):
+                    width = cols.stop - cols.start
+                    bank = psum.tile([P, width], F32, name="bank%d_%d" % (t, n))
+                    nc.tensor.matmul_mx(
+                        out=bank[:],
+                        lhsT=w_codes[:, t, :].bitcast(FP8X4),
+                        lhsT_scale=w_plane[:, t, :],
+                        rhs=codes[:, cols].bitcast(FP8X4),
+                        rhs_scale=plane[:, cols],
+                        start=True,
+                        stop=True,
+                    )
+                    nc.scalar.activation(row[:, cols], bank[:], COPY, scale=scale)
+                rows.append(row)
+            return rows
+
+        def regroup(grouped, placed, t, factor):
+            last = t == PACK - 1
+            for n, cols in enumerate(halves):
+                if n == 0 and last:
+                    if factor is None:
+                        nc.vector.tensor_copy(grouped[n][:, :, t], placed[:, cols])
+                    else:
+                        nc.vector.tensor_scalar(grouped[n][:, :, t], placed[:, cols], factor, None, MULT)
+                    continue
+                if n == 0 and t == PACK - 2:
+                    target = grouped[n][:, :, t : t + 2]
+                    source = placed[:, cols].unsqueeze(2).to_broadcast([P, HALF, 2])
+                else:
+                    target = grouped[n][:, :, t]
+                    source = placed[:, cols]
+                nc.scalar.activation(target, source, COPY, scale=1.0 if factor is None else factor)
+
+        def quantise(name, grouped):
+            codes = new(name + "_codes", [P, S], U32)
+            plane = new(name + "_plane", [P, S], U8)
+            for n, cols in enumerate(halves):
+                nc.vector.quantize_mx(
+                    out=codes[:, cols].bitcast(FP8X4), scales=plane[:, cols], in_=grouped[n][:].rearrange("p c t -> p (c t)")
+                )
+            return codes, plane
+
+        def pipeline(first, second, put_first, put_second):
+            first(0)
+            second(0)
+            for t in range(1, PACK):
+                first(t)
+                put_first(t - 1)
+                second(t)
+                put_second(t - 1)
+            put_first(PACK - 1)
+            put_second(PACK - 1)
+
+        y = product("y", w1_codes, w1_plane, x_codes, x_plane, 1.0)
+        nc.sync.dma_start(out=w_raw[:], in_=as_words(w2_words))
+        load_scale_rows([nc.sync] * 4, w_raw_scales, w2_scales)
+        w2_plane = deal("w2_plane", w_raw_scales, U8)
+        w2_codes = deal("w2_codes", w_raw, I32)
+
+        a = [new("a%d" % t, [P, V], F32) for t in range(PACK)]
+        b = [new("b%d" % t, [P, V], F32) for t in range(PACK)]
+        d2 = [new("d2_%d" % t, [P, S], F32) for t in range(PACK)]
+        z = [new("z%d" % n, [P, HALF, PACK], BF16) for n in range(2)]
+
+        def put_product(t):
+            nc.vector.tensor_tensor(d2[t][:].indirect(lb_sb[:]), a[t][:], b[t][:], MULT)
+            regroup(z, d2[t], t, gain[:, t : t + 1])
+
+        pipeline(
+            lambda t: nc.vector.tensor_copy(a[t][:], y[t][:].indirect(la_sb[:])),
+            lambda t: nc.vector.tensor_copy(b[t][:], y[t][:].indirect(lb_sb[:])),
+            lambda t: nc.vector.tensor_tensor(d2[t][:].indirect(la_sb[:]), a[t][:], b[t][:], ADD),
+            put_product,
+        )
+        z_codes, z_plane = quantise("z", z)
+
+        minus_h = product("minus_h", w2_codes, w2_plane, z_codes, z_plane, -1.0)
+
+        minus_c = [new("minus_c%d" % t, [P, V], F32) for t in range(PACK)]
+        twice_c = [new("twice_c%d" % t, [P, V], F32) for t in range(PACK)]
+        minus_sum = [new("minus_sum%d" % t, [P, V], F32) for t in range(PACK)]
+        size = [new("size%d" % t, [P, V], F32) for t in range(PACK)]
+        result = [new("result%d" % t, [P, S], F32) for t in range(PACK)]
+        rounded = [new("rounded%d" % n, [P, HALF, PACK], BF16) for n in range(2)]
+        out_rows = out_0.rearrange("(p t) j -> p t j", t=PACK)
+
+        def fetch_c(t):
+            nc.vector.tensor_copy(minus_c[t][:], minus_h[t][:].indirect(ma_sb[:]))
+            nc.scalar.activation(twice_c[t][:], minus_c[t][:], COPY, scale=-2.0)
+
+        def fetch_sum(t):
+            nc.vector.tensor_tensor(minus_sum[t][:], minus_h[t][:].indirect(mb_sb[:]), minus_c[t][:], ADD)
+            nc.scalar.activation(size[t][:], minus_sum[t][:], ABS)
+
+        def put_size(t):
+            nc.vector.tensor_copy(result[t][:].indirect(ma_sb[:]), size[t][:])
+            nc.sync.dma_start(out=out_rows[:, t, :], in_=result[t][:])
+            regroup(rounded, result[t], t, None)
+
+        pipeline(
+            fetch_c,
+            fetch_sum,
+            lambda t: nc.vector.tensor_tensor(result[t][:].indirect(mb_sb[:]), minus_sum[t][:], twice_c[t][:], ADD),
+            put_size,
+        )
+        out_codes, out_plane = quantise("out", rounded)
+
+        out_words = as_words(out_1)
+        for cols in halves:
+            nc.sync.dma_start(out=out_words[:, cols], in_=out_codes[:, cols].bitcast(I32))
+        for q in range(4):
+            queue = nc.scalar if q % 2 else nc.sync
+            queue.dma_start(out=out_2[0, 4 * q : 4 * q + 4, :].bitcast(I32), in_=out_plane[32 * q : 32 * q + 4, :].bitcast(I32))

@@ -32,8 +32,8 @@ def tile_picked_pairpoly_none_po_kernel(
     def as_words(packed):
         return packed[0].rearrange("p n t -> p (n t)").bitcast(I32)
 
-    def load_scale_rows(queues, plane, rows):
-        for q, queue in enumerate(queues):
+    def load_scale_rows(queue, plane, rows, quadrants):
+        for q in quadrants:
             queue.dma_start(out=plane[32 * q : 32 * q + 4, :].bitcast(I32), in_=rows[0, 4 * q : 4 * q + 4, :].bitcast(I32))
 
     with ExitStack() as ctx:
@@ -52,34 +52,35 @@ def tile_picked_pairpoly_none_po_kernel(
         x_table_scales = new("x_table_scales", [P, T], U8)
         w_raw = new("w_raw", [P, S], I32)
         w_raw_scales = new("w_raw_scales", [P, S], U8)
-        gain = new("gain", [P, PACK], F32)
 
         nc.vector.memset(x_table_scales[:].bitcast(I32), 0)
-        nc.gpsimd.memset(w_raw_scales[:].bitcast(I32), 0)
+        nc.vector.memset(w_raw_scales[:].bitcast(I32), 0)
 
         nc.sync.dma_start(offs_sb[:], offs)
         nc.sync.dma_start(la_sb[:], la)
         nc.sync.dma_start(lb_sb[:], lb)
-        nc.sync.dma_start(ma_sb[:], ma)
-        nc.sync.dma_start(mb_sb[:], mb)
+        load_scale_rows(nc.sync, x_table_scales, x_scales, (0, 1, 2, 3))
         nc.sync.dma_start(out=x_table[:].bitcast(I32), in_=as_words(x_words))
         nc.sync.dma_start(out=w_raw[:], in_=as_words(w1_words))
-        load_scale_rows([nc.scalar] * 4, x_table_scales, x_scales)
-        load_scale_rows([nc.scalar, nc.scalar, nc.gpsimd, nc.gpsimd], w_raw_scales, w1_scales)
-        nc.gpsimd.dma_start(out=gain[:], in_=gn.rearrange("(p t) o -> p (t o)", t=PACK))
+        load_scale_rows(nc.sync, w_raw_scales, w1_scales, (0, 1, 2, 3))
+        nc.sync.dma_start(ma_sb[:], ma)
+        nc.sync.dma_start(mb_sb[:], mb)
 
-        def deal(name, raw, dtype):
-            dealt = new(name, [P, PACK, P], dtype)
-            nc.vector.tensor_copy(out=dealt[:].rearrange("p t m -> p m t"), in_=raw[:].rearrange("p (m t) -> p m t", t=PACK))
-            return dealt
+        def deal(name, raw, dtype, first, count, tag):
+            dealt = held.tile([P, count, P], dtype, name=name, tag=tag, align_bytes=64)
+            source = raw[:].rearrange("p (m t) -> p m t", t=PACK)[:, :, first : first + count]
+            nc.vector.tensor_copy(out=dealt[:].rearrange("p t m -> p m t"), in_=source)
+            return [dealt[:, t, :] for t in range(count)]
 
         x_codes = new("x_codes", [P, S], U32)
         x_plane = new("x_plane", [P, S], U8)
-        w1_plane = deal("w1_plane", w_raw_scales, U8)
         nc.vector.tensor_copy(x_plane[:], x_table_scales[:].indirect(offs_sb[:]))
         nc.vector.tensor_copy(x_codes[:, halves[0]], x_table[:].indirect(offs_sb[:, 0 : HALF // 16]))
-        w1_codes = deal("w1_codes", w_raw, I32)
+        w1_codes = deal("w1_codes_first", w_raw, I32, 0, 1, "w1_codes_first")
+        w1_plane = deal("w1_plane_first", w_raw_scales, U8, 0, 1, "x_table_scales")
         nc.vector.tensor_copy(x_codes[:, halves[1]], x_table[:].indirect(offs_sb[:, HALF // 16 : S // 16]))
+        w1_codes = w1_codes + deal("w1_codes_rest", w_raw, I32, 1, PACK - 1, "x_table")
+        w1_plane = w1_plane + deal("w1_plane_rest", w_raw_scales, U8, 1, PACK - 1, "w1_plane_rest")
 
         def product(name, w_codes, w_plane, codes, plane, scale):
             rows = []
@@ -90,8 +91,8 @@ def tile_picked_pairpoly_none_po_kernel(
                     bank = psum.tile([P, width], F32, name="bank%d_%d" % (t, n))
                     nc.tensor.matmul_mx(
                         out=bank[:],
-                        lhsT=w_codes[:, t, :].bitcast(FP8X4),
-                        lhsT_scale=w_plane[:, t, :],
+                        lhsT=w_codes[t].bitcast(FP8X4),
+                        lhsT_scale=w_plane[t],
                         rhs=codes[:, cols].bitcast(FP8X4),
                         rhs_scale=plane[:, cols],
                         start=True,
@@ -127,7 +128,7 @@ def tile_picked_pairpoly_none_po_kernel(
                 )
             return codes, plane
 
-        def pipeline(first, second, put_first, put_second):
+        def pipeline(first, second, put_first, put_second, between):
             first(0)
             second(0)
             for t in range(1, PACK):
@@ -136,18 +137,26 @@ def tile_picked_pairpoly_none_po_kernel(
                 second(t)
                 put_second(t - 1)
             put_first(PACK - 1)
+            between()
             put_second(PACK - 1)
 
+        gain = held.tile([P, PACK], F32, name="gain", tag="w1_codes_first", align_bytes=64)
         y = product("y", w1_codes, w1_plane, x_codes, x_plane, 1.0)
         nc.sync.dma_start(out=w_raw[:], in_=as_words(w2_words))
-        load_scale_rows([nc.sync] * 4, w_raw_scales, w2_scales)
-        w2_plane = deal("w2_plane", w_raw_scales, U8)
-        w2_codes = deal("w2_codes", w_raw, I32)
+        load_scale_rows(nc.sync, w_raw_scales, w2_scales, (0, 1, 2, 3))
+        nc.sync.dma_start(out=gain[:], in_=gn.rearrange("(p t) o -> p (t o)", t=PACK))
 
         a = [new("a%d" % t, [P, V], F32) for t in range(PACK)]
         b = [new("b%d" % t, [P, V], F32) for t in range(PACK)]
         d2 = [new("d2_%d" % t, [P, S], F32) for t in range(PACK)]
         z = [new("z%d" % n, [P, HALF, PACK], BF16) for n in range(2)]
+
+        w2_codes = []
+        w2_plane = []
+
+        def deal_first_of_w2():
+            w2_codes.extend(deal("w2_codes_first", w_raw, I32, 0, 1, "y3"))
+            w2_plane.extend(deal("w2_plane_first", w_raw_scales, U8, 0, 1, "a2"))
 
         def put_product(t):
             nc.vector.tensor_tensor(d2[t][:].indirect(lb_sb[:]), a[t][:], b[t][:], MULT)
@@ -158,8 +167,11 @@ def tile_picked_pairpoly_none_po_kernel(
             lambda t: nc.vector.tensor_copy(b[t][:], y[t][:].indirect(lb_sb[:])),
             lambda t: nc.vector.tensor_tensor(d2[t][:].indirect(la_sb[:]), a[t][:], b[t][:], ADD),
             put_product,
+            deal_first_of_w2,
         )
         z_codes, z_plane = quantise("z", z)
+        w2_codes.extend(deal("w2_codes_rest", w_raw, I32, 1, PACK - 1, "z0"))
+        w2_plane.extend(deal("w2_plane_rest", w_raw_scales, U8, 1, PACK - 1, "z1"))
 
         minus_h = product("minus_h", w2_codes, w2_plane, z_codes, z_plane, -1.0)
 
@@ -189,6 +201,7 @@ def tile_picked_pairpoly_none_po_kernel(
             fetch_sum,
             lambda t: nc.vector.tensor_tensor(result[t][:].indirect(mb_sb[:]), minus_sum[t][:], twice_c[t][:], ADD),
             put_size,
+            lambda: None,
         )
         out_codes, out_plane = quantise("out", rounded)
 

from contextlib import ExitStack

import concourse.mybir as mybir

F32 = mybir.dt.float32
BF16 = mybir.dt.bfloat16
I32 = mybir.dt.int32
U32 = mybir.dt.uint32
U16 = mybir.dt.uint16
U8 = mybir.dt.uint8
FP8X4 = mybir.dt.float8_e4m3fn_x4
ADD = mybir.AluOpType.add
MULT = mybir.AluOpType.mult
COPY = mybir.ActivationFunctionType.Copy
ABS = mybir.ActivationFunctionType.Abs

P = 128
PACK = 4
T = 2048
S = 512
V = 256
HALF = S // 2
FLOPS = 2 * 512 * 512 * 512 * 2


def tile_picked_pairpoly_none_po_kernel(
    tc, x_words, x_scales, w1_words, w1_scales, gn, w2_words, w2_scales, offs, la, lb, ma, mb, out_0, out_1, out_2
):
    nc = tc.nc
    halves = [slice(0, HALF), slice(HALF, S)]

    def as_words(packed):
        return packed[0].rearrange("p n t -> p (n t)").bitcast(I32)

    def load_scale_rows(queue, plane, rows, quadrants):
        for q in quadrants:
            queue.dma_start(out=plane[32 * q : 32 * q + 4, :].bitcast(I32), in_=rows[0, 4 * q : 4 * q + 4, :].bitcast(I32))

    with ExitStack() as ctx:
        held = ctx.enter_context(tc.tile_pool(name="held", bufs=1))
        psum = ctx.enter_context(tc.psum_pool(name="psum", bufs=1))

        def new(name, shape, dtype):
            return held.tile(shape, dtype, name=name, align_bytes=64)

        offs_sb = new("offs_sb", [P, S // 16], U16)
        la_sb = new("la_sb", [P, V // 16], U16)
        lb_sb = new("lb_sb", [P, V // 16], U16)
        ma_sb = new("ma_sb", [P, V // 16], U16)
        mb_sb = new("mb_sb", [P, V // 16], U16)
        x_table = new("x_table", [P, T], U32)
        x_table_scales = new("x_table_scales", [P, T], U8)
        w_raw = new("w_raw", [P, S], I32)
        w_raw_scales = new("w_raw_scales", [P, S], U8)

        nc.vector.memset(x_table_scales[:].bitcast(I32), 0)
        nc.vector.memset(w_raw_scales[:].bitcast(I32), 0)

        nc.sync.dma_start(offs_sb[:], offs)
        nc.sync.dma_start(la_sb[:], la)
        nc.sync.dma_start(lb_sb[:], lb)
        load_scale_rows(nc.sync, x_table_scales, x_scales, (0, 1, 2, 3))
        nc.sync.dma_start(out=x_table[:].bitcast(I32), in_=as_words(x_words))
        nc.sync.dma_start(out=w_raw[:], in_=as_words(w1_words))
        load_scale_rows(nc.sync, w_raw_scales, w1_scales, (0, 1, 2, 3))
        nc.sync.dma_start(ma_sb[:], ma)
        nc.sync.dma_start(mb_sb[:], mb)

        def deal(name, raw, dtype, first, count, tag):
            dealt = held.tile([P, count, P], dtype, name=name, tag=tag, align_bytes=64)
            source = raw[:].rearrange("p (m t) -> p m t", t=PACK)[:, :, first : first + count]
            nc.vector.tensor_copy(out=dealt[:].rearrange("p t m -> p m t"), in_=source)
            return [dealt[:, t, :] for t in range(count)]

        x_codes = new("x_codes", [P, S], U32)
        x_plane = new("x_plane", [P, S], U8)
        nc.vector.tensor_copy(x_plane[:], x_table_scales[:].indirect(offs_sb[:]))
        nc.vector.tensor_copy(x_codes[:, halves[0]], x_table[:].indirect(offs_sb[:, 0 : HALF // 16]))
        w1_codes = deal("w1_codes_first", w_raw, I32, 0, 1, "w1_codes_first")
        w1_plane = deal("w1_plane_first", w_raw_scales, U8, 0, 1, "x_table_scales")
        nc.vector.tensor_copy(x_codes[:, halves[1]], x_table[:].indirect(offs_sb[:, HALF // 16 : S // 16]))
        w1_codes = w1_codes + deal("w1_codes_rest", w_raw, I32, 1, PACK - 1, "x_table")
        w1_plane = w1_plane + deal("w1_plane_rest", w_raw_scales, U8, 1, PACK - 1, "w1_plane_rest")

        def product(name, w_codes, w_plane, codes, plane, scale):
            rows = []
            for t in range(PACK):
                row = new("%s%d" % (name, t), [P, S], F32)
                for n, cols in enumerate(halves if t == 0 else [slice(0, S)]):
                    width = cols.stop - cols.start
                    bank = psum.tile([P, width], F32, name="bank%d_%d" % (t, n))
                    nc.tensor.matmul_mx(
                        out=bank[:],
                        lhsT=w_codes[t].bitcast(FP8X4),
                        lhsT_scale=w_plane[t],
                        rhs=codes[:, cols].bitcast(FP8X4),
                        rhs_scale=plane[:, cols],
                        start=True,
                        stop=True,
                    )
                    nc.scalar.activation(row[:, cols], bank[:], COPY, scale=scale)
                rows.append(row)
            return rows

        def regroup(grouped, placed, t, factor):
            last = t == PACK - 1
            for n, cols in enumerate(halves):
                if n == 0 and last:
                    if factor is None:
                        nc.vector.tensor_copy(grouped[n][:, :, t], placed[:, cols])
                    else:
                        nc.vector.tensor_scalar(grouped[n][:, :, t], placed[:, cols], factor, None, MULT)
                    continue
                if n == 0 and t == PACK - 2:
                    target = grouped[n][:, :, t : t + 2]
                    source = placed[:, cols].unsqueeze(2).to_broadcast([P, HALF, 2])
                else:
                    target = grouped[n][:, :, t]
                    source = placed[:, cols]
                nc.scalar.activation(target, source, COPY, scale=1.0 if factor is None else factor)

        def quantise(name, grouped):
            codes = new(name + "_codes", [P, S], U32)
            plane = new(name + "_plane", [P, S], U8)
            for n, cols in enumerate(halves):
                nc.vector.quantize_mx(
                    out=codes[:, cols].bitcast(FP8X4), scales=plane[:, cols], in_=grouped[n][:].rearrange("p c t -> p (c t)")
                )
            return codes, plane

        def pipeline(first, second, put_first, put_second, between):
            first(0)
            second(0)
            for t in range(1, PACK):
                first(t)
                put_first(t - 1)
                second(t)
                put_second(t - 1)
            put_first(PACK - 1)
            between()
            put_second(PACK - 1)

        gain = held.tile([P, PACK], F32, name="gain", tag="w1_codes_first", align_bytes=64)
        y = product("y", w1_codes, w1_plane, x_codes, x_plane, 1.0)
        nc.sync.dma_start(out=w_raw[:], in_=as_words(w2_words))
        load_scale_rows(nc.sync, w_raw_scales, w2_scales, (0, 1, 2, 3))
        nc.sync.dma_start(out=gain[:], in_=gn.rearrange("(p t) o -> p (t o)", t=PACK))

        a = [new("a%d" % t, [P, V], F32) for t in range(PACK)]
        b = [new("b%d" % t, [P, V], F32) for t in range(PACK)]
        d2 = [new("d2_%d" % t, [P, S], F32) for t in range(PACK)]
        z = [new("z%d" % n, [P, HALF, PACK], BF16) for n in range(2)]

        w2_codes = []
        w2_plane = []

        def deal_first_of_w2():
            w2_codes.extend(deal("w2_codes_first", w_raw, I32, 0, 1, "y3"))
            w2_plane.extend(deal("w2_plane_first", w_raw_scales, U8, 0, 1, "a2"))

        def put_product(t):
            nc.vector.tensor_tensor(d2[t][:].indirect(lb_sb[:]), a[t][:], b[t][:], MULT)
            regroup(z, d2[t], t, gain[:, t : t + 1])

        pipeline(
            lambda t: nc.vector.tensor_copy(a[t][:], y[t][:].indirect(la_sb[:])),
            lambda t: nc.vector.tensor_copy(b[t][:], y[t][:].indirect(lb_sb[:])),
            lambda t: nc.vector.tensor_tensor(d2[t][:].indirect(la_sb[:]), a[t][:], b[t][:], ADD),
            put_product,
            deal_first_of_w2,
        )
        z_codes, z_plane = quantise("z", z)
        w2_codes.extend(deal("w2_codes_rest", w_raw, I32, 1, PACK - 1, "z0"))
        w2_plane.extend(deal("w2_plane_rest", w_raw_scales, U8, 1, PACK - 1, "z1"))

        minus_h = product("minus_h", w2_codes, w2_plane, z_codes, z_plane, -1.0)

        minus_c = [new("minus_c%d" % t, [P, V], F32) for t in range(PACK)]
        twice_c = [new("twice_c%d" % t, [P, V], F32) for t in range(PACK)]
        minus_sum = [new("minus_sum%d" % t, [P, V], F32) for t in range(PACK)]
        size = [new("size%d" % t, [P, V], F32) for t in range(PACK)]
        result = [new("result%d" % t, [P, S], F32) for t in range(PACK)]
        rounded = [new("rounded%d" % n, [P, HALF, PACK], BF16) for n in range(2)]
        out_rows = out_0.rearrange("(p t) j -> p t j", t=PACK)

        def fetch_c(t):
            nc.vector.tensor_copy(minus_c[t][:], minus_h[t][:].indirect(ma_sb[:]))
            nc.scalar.activation(twice_c[t][:], minus_c[t][:], COPY, scale=-2.0)

        def fetch_sum(t):
            nc.vector.tensor_tensor(minus_sum[t][:], minus_h[t][:].indirect(mb_sb[:]), minus_c[t][:], ADD)
            nc.scalar.activation(size[t][:], minus_sum[t][:], ABS)

        def put_size(t):
            nc.vector.tensor_copy(result[t][:].indirect(ma_sb[:]), size[t][:])
            nc.sync.dma_start(out=out_rows[:, t, :], in_=result[t][:])
            regroup(rounded, result[t], t, None)

        pipeline(
            fetch_c,
            fetch_sum,
            lambda t: nc.vector.tensor_tensor(result[t][:].indirect(mb_sb[:]), minus_sum[t][:], twice_c[t][:], ADD),
            put_size,
            lambda: None,
        )
        out_codes, out_plane = quantise("out", rounded)

        out_words = as_words(out_1)
        for cols in halves:
            nc.sync.dma_start(out=out_words[:, cols], in_=out_codes[:, cols].bitcast(I32))
        for q in range(4):
            queue = nc.scalar if q % 2 else nc.sync
            queue.dma_start(out=out_2[0, 4 * q : 4 * q + 4, :].bitcast(I32), in_=out_plane[32 * q : 32 * q + 4, :].bitcast(I32))
